import numpy as np
import ml_dtypes


def mxq(x, axis, fmt="e4m3"):
    dtype, down = {"e4m3": (ml_dtypes.float8_e4m3fn, 7), "e5m2": (ml_dtypes.float8_e5m2, 14)}[fmt]
    v = np.moveaxis(np.asarray(x, np.float32).astype(ml_dtypes.bfloat16).astype(np.float64), axis, -1)
    blocks = v.reshape(v.shape[:-1] + (-1, 32))
    amax = np.abs(blocks).max(-1, keepdims=True)
    byte = np.maximum(np.where(amax > 0, np.frexp(amax)[1] - 1 + 127, 0) - down, 1)
    scale = np.exp2(byte - 127.0)
    codes = (blocks / scale).astype(np.float32).astype(dtype).astype(np.float64)
    return np.moveaxis((codes * scale).reshape(v.shape), -1, axis)


WIDE = False


def mx_kscale(k):
    if not WIDE:
        return np.ones(k)
    levels = np.array([10, -10, 5, -5, 0])
    if k % 512:
        return np.exp2(np.random.permutation(np.resize(levels, k // 32))).repeat(32)
    a = np.empty((k // 512, 16))
    for p in range(k // 512):
        a[p, :8] = np.random.permutation(np.resize(levels, 8))
        for g in range(8):
            far = levels[np.abs(levels - a[p, g]) >= 10]
            a[p, g + 8] = far[np.random.randint(len(far))]
    return np.exp2(a.ravel()).repeat(32)


def f64(x):
    return np.asarray(x).astype(np.float64)


def striped(idx):
    return np.tile(np.asarray(idx).reshape(-1, 16).T, (8, 1)).astype(np.uint16)


def unstriped(offs):
    return offs[:16].T.reshape(-1).astype(np.int64)


E2M1 = np.array([0.0, 0.5, 1.0, 1.5, 2.0, 3.0, 4.0, 6.0, -0.0, -0.5, -1.0, -1.5, -2.0, -3.0, -4.0, -6.0])


def pack_weight(w, fmt):
    k, n = w.shape
    w = f64(np.asarray(w, np.float32).astype(ml_dtypes.bfloat16)).reshape(k // 32, 32, n)
    amax = np.abs(w).max(1)
    if fmt == "e4m3":
        byte = np.frexp(amax)[1] - 1 + 127 - 7
    else:
        mant, ex = np.frexp(amax / 6.0)
        byte = np.where(mant > 0.5, ex, ex - 1) + 127
    byte = np.clip(np.where(amax > 0, byte, 1), 1, 254)
    scaled = (w * np.exp2(127.0 - byte)[:, None, :]).reshape(k, n).astype(np.float32)
    by_word = np.ascontiguousarray(scaled.reshape(k // 512, 128, 4, n).transpose(0, 1, 3, 2))
    if fmt == "e4m3":
        words = by_word.astype(ml_dtypes.float8_e4m3fn).view(np.uint8)
    else:
        c = by_word.astype(ml_dtypes.float4_e2m1fn).view(np.uint8) & 0xF
        words = (c[..., 0::2] | (c[..., 1::2] << 4)).reshape(k // 512, 128, 2 * n)
    return np.ascontiguousarray(words), np.ascontiguousarray(byte.astype(np.uint8).reshape(k // 512, 16, n))


def unpack_weight(words, scales, fmt):
    g, _, n = scales.shape
    words = np.ascontiguousarray(words).reshape(g, 128, n, -1)
    if fmt == "e4m3":
        vals = words.view(ml_dtypes.float8_e4m3fn).astype(np.float64)
    else:
        nib = np.empty((g, 128, n, 4), np.uint8)
        nib[..., 0::2] = words & 0xF
        nib[..., 1::2] = words >> 4
        vals = E2M1[nib]
    vals = vals * np.repeat(np.exp2(scales.astype(np.float64) - 127.0), 8, axis=1)[..., None]
    return vals.transpose(0, 1, 3, 2).reshape(g * 512, n)


def bf(x):
    return np.asarray(x, np.float32).astype(ml_dtypes.bfloat16)


def planes(Y):
    r, m = Y.shape
    b = f64(bf(Y)).reshape(r // 32, 32, m)
    amax = np.abs(b).max(1)
    byte = np.clip(np.where(amax > 0, np.frexp(amax)[1] - 1 + 127 - 7, 1), 1, 254)
    codes = (b * np.exp2(127.0 - byte)[:, None, :]).reshape(r, m).astype(np.float32).astype(ml_dtypes.float8_e4m3fn).view(np.uint8)
    words = codes.reshape(r // 512, 128, 4, m).transpose(0, 1, 3, 2)
    return np.ascontiguousarray(words), np.ascontiguousarray(byte.astype(np.uint8).reshape(r // 512, 16, m))


D, T, I, Q, E, V, G = 512, 2048, 512, 256, 512, 32, 64


def setup_inputs():
    n = np.random.standard_normal
    idx = np.random.permutation(T)[:I]
    idx2 = np.random.permutation(T)[:I]
    fd = mx_kscale(D)
    fi = mx_kscale(I)
    ti = np.ones(T)
    ti[idx] = fi
    keysp = pack_weight(n((D, T)) / fd[:, None], "e2m1")
    return {
        "query": (n((D, Q)) * 0.9 / np.sqrt(D) * fd[:, None]).astype(np.float32),
        "keys_words": keysp[0],
        "keys_scales": keysp[1],
        "lam": (np.random.uniform(0.5, 1.5, (1, Q))).astype(np.float32),
        "cap": (np.random.uniform(0.01, 0.018, (Q, 1))).astype(np.float32),
        "os": (np.random.uniform(4.0, 16.0, (1, I)) * fi).astype(np.float32),
        "vals": (n((E, T)) / ti).astype(np.float32),
        "offs": striped(idx),
        "offs2": striped(idx2),
    }


def reference(query, keys_words, keys_scales, lam, cap, os, vals, offs, offs2):
    idx = unstriped(offs)
    idx2 = unstriped(offs2)
    keysu = unpack_weight(keys_words, keys_scales, "e2m1")
    keysidxg = keysu[:, idx]
    queryq = mxq(f64(query), 0, "e4m3")
    a0 = keysidxg.T @ queryq
    keysidx2g = keysu[:, idx2]
    b0 = keysidx2g.T @ queryq
    vo = np.tanh(a0 - b0)
    vg = vo.reshape(I, V, Q // V).mean(axis=2)
    vr = np.repeat(vg, Q // V, axis=1)
    s0 = a0 + vr * f64(lam)
    s = s0.T
    p = np.exp(s - np.max(s, axis=1, keepdims=True))
    r = p / np.sum(p, axis=1, keepdims=True)
    pg = r.reshape(Q, G, I // G).sum(axis=2)
    k0 = np.minimum(pg, f64(cap)) / pg
    kr = np.repeat(k0, I // G, axis=1)
    w = r * kr
    wo1 = w * f64(os)
    wt1 = wo1.T
    vt1 = f64(vals)[:, idx].T
    vt1q = mxq(vt1, 0, "e4m3")
    wt1q = mxq(wt1, 0, "e4m3")
    o = vt1q.T @ wt1q
    words, scales = planes(o)
    return o, words, scales

@@ -1,0 +1,314 @@
+from contextlib import ExitStack
+
+import concourse.mybir as mybir
+from concourse.masks import make_identity
+
+D, T, I, Q, E = 512, 2048, 512, 256, 512
+FLOPS = 3 * 2 * 512 * 512 * 256
+
+F32 = mybir.dt.float32
+BF16 = mybir.dt.bfloat16
+I32 = mybir.dt.int32
+U32 = mybir.dt.uint32
+U16 = mybir.dt.uint16
+U8 = mybir.dt.uint8
+FP8X4 = mybir.dt.float8_e4m3fn_x4
+FP4X4 = mybir.dt.float4_e2m1fn_x4
+ALU = mybir.AluOpType
+ACT = mybir.ActivationFunctionType
+AXIS = mybir.AxisListType
+
+P = 128
+PACK = 4
+BANK = 512
+HALF = I // 2
+RUNS = 64
+
+
+def tile_attend_groupvotes_runcap_read_pl_kernel(
+    tc, query, keys_words, keys_scales, lam, cap, slot_factor, vals, offs, offs2, out_0, out_1, out_2
+):
+    nc = tc.nc
+    with ExitStack() as ctx:
+        sb = ctx.enter_context(tc.tile_pool(name="sb", bufs=1))
+        ps = ctx.enter_context(tc.psum_pool(name="ps", bufs=1))
+
+        def sbuf(name, shape, dtype, tag=None):
+            return sb.tile(shape, dtype, name=name, tag=tag or name, align_bytes=64)
+
+        def bank(name, number):
+            return ps.tile([P, BANK], F32, name=name, tag="bank%d" % number)
+
+        list_a = sb.tile([P, I // 16], U16, name="list_a")
+        list_b = sb.tile([P, I // 16], U16, name="list_b")
+        pool_words = sbuf("pool_words", [P, T], U16)
+        pool_scales = sbuf("pool_scales", [P, T], U8)
+        q_raw = sbuf("q_raw", [P, PACK, Q], F32)
+        nc.gpsimd.memset(pool_scales[:].bitcast(I32), 0)
+        nc.sync.dma_start(list_a[:], offs)
+        nc.sync.dma_start(list_b[:], offs2)
+        for quad in range(4):
+            nc.sync.dma_start(
+                pool_scales[32 * quad : 32 * quad + 4, :].bitcast(I32),
+                keys_scales[0][4 * quad : 4 * quad + 4, :].bitcast(I32),
+            )
+        nc.sync.dma_start(q_raw[:], query.rearrange("(p j) q -> p j q", j=PACK))
+        nc.sync.dma_start(pool_words[:].bitcast(I32), keys_words[0].bitcast(I32))
+        val_rows = vals.rearrange("(p j) t -> j p t", j=PACK)
+        val_pool = [sbuf("val_pool%d" % j, [P, T], F32) for j in range(PACK)]
+        row_raw = sbuf("row_raw", [2, Q], F32)
+        os_col = sbuf("os_col", [P, PACK], F32)
+        nc.sync.dma_start(val_pool[0][:], val_rows[0])
+        nc.sync.dma_start(row_raw[0:1, :], lam)
+        nc.sync.dma_start(row_raw[1:2, :], cap.rearrange("q o -> o q"))
+        nc.sync.dma_start(os_col[:], slot_factor.rearrange("o (p t) -> (o p) t", t=PACK))
+        for j in range(1, PACK):
+            nc.sync.dma_start(val_pool[j][:], val_rows[j])
+
+        ident = sbuf("ident", [P, P], F32)
+        make_identity(nc, ident[:])
+        row_dealt = sbuf("row_dealt", [P, Q], F32)
+        nc.gpsimd.memset(row_dealt[:], 0.0)
+
+        words_a = sbuf("words_a", [P, I], U16)
+        scales_a = sbuf("scales_a", [P, I], U8)
+        scales_b = sbuf("scales_b", [P, I], U8)
+        nc.vector.tensor_copy(scales_a[:], pool_scales[:].indirect(list_a[:]))
+        nc.vector.tensor_copy(scales_b[:], pool_scales[:].indirect(list_b[:]))
+
+        q_bf = sbuf("q_bf", [P, 2, P, PACK], BF16)
+        q_src = q_raw[:].rearrange("p j (v h r) -> p h v j r", h=2, r=4)
+        for h in range(2):
+            nc.scalar.copy(q_bf[:, h].rearrange("p (v r) j -> p v j r", r=4), q_src[:, h])
+        q_codes = sbuf("q_codes", [P, Q], U32)
+        q_scales = sbuf("q_scales", [P, Q], U8)
+        nc.vector.quantize_mx(
+            out=q_codes[:].bitcast(FP8X4), scales=q_scales[:], in_=q_bf[:].rearrange("p h m j -> p (h m j)")
+        )
+
+        def scores(out, h, words, scales):
+            cols = slice(h * P, (h + 1) * P)
+            nc.tensor.matmul_mx(
+                out=out,
+                lhsT=q_codes[:, cols].bitcast(FP8X4),
+                lhsT_scale=q_scales[:, cols],
+                rhs=words.bitcast(FP4X4),
+                rhs_scale=scales,
+                start=True,
+                stop=True,
+            )
+
+        nc.vector.tensor_copy(words_a[:], pool_words[:].indirect(list_a[:]))
+        a0 = sbuf("a0", [P, 2, I], F32)
+        for s in range(2):
+            a_bank = bank("a_bank%d" % s, s)
+            slots = slice(s * HALF, (s + 1) * HALF)
+            for h in range(2):
+                scores(a_bank[:, h * HALF : (h + 1) * HALF], h, words_a[:, slots], scales_a[:, slots])
+            nc.scalar.copy(a0[:, :, slots], a_bank[:].rearrange("p (h i) -> p h i", h=2))
+
+        nc.gpsimd.tensor_copy(
+            row_dealt[0:2, :].rearrange("p (h v r) -> p h v r", h=2, r=4),
+            row_raw[:].rearrange("p (v h r) -> p h v r", h=2, r=4),
+        )
+        row_bank = bank("row_bank", 6)
+        for h in range(2):
+            nc.tensor.transpose(row_bank[:, h * P : (h + 1) * P], row_dealt[:, h * P : (h + 1) * P], ident[:])
+        lam_cap = sbuf("lam_cap", [P, 2, 2], F32)
+        nc.scalar.copy(lam_cap[:], row_bank[:, 0:Q].rearrange("p (h c) -> p h c", h=2)[:, :, 0:2])
+
+        v_codes = [sbuf("v_codes%d" % j, [P, P], U32) for j in range(PACK)]
+        v_scales = [sbuf("v_scales%d" % j, [P, P], U8) for j in range(PACK)]
+        v_bf = [sbuf("v_bf%d" % j, [P, P, PACK], BF16) for j in range(PACK)]
+
+        def gather_values(j):
+            picked = sbuf("picked%d" % j, [P, I], BF16, tag=("diff0", "diff1", "picked2", "picked3")[j])
+            if j == 0:
+                nc.vector.tensor_copy(picked[:], val_pool[j][:].indirect(list_a[:]))
+            else:
+                nc.scalar.activation(picked[:], val_pool[j][:].indirect(list_a[:]), ACT.Copy)
+            pairs = picked[:].bitcast(F32)
+            turned = bank("turned%d" % j, 7)
+            for u in range(2):
+                nc.tensor.transpose(turned[:, u * P : (u + 1) * P], pairs[:, u : I // 2 : 2], ident[:])
+            nc.scalar.copy(
+                v_bf[j][:].rearrange("p m t -> p (m t)").bitcast(F32).rearrange("p (m u) -> p m u", u=2),
+                turned[:, 0 : 2 * P].rearrange("p (u m) -> p m u", u=2),
+            )
+
+        def quantize_values(j):
+            nc.vector.quantize_mx(
+                out=v_codes[j][:].bitcast(FP8X4), scales=v_scales[j][:], in_=v_bf[j][:].rearrange("p m t -> p (m t)")
+            )
+
+        votes = [sbuf("votes%d" % s, [P, 2, HALF], F32) for s in range(2)]
+        vote_bank = bank("vote_bank", 6)
+
+        def opponents(s):
+            words_b = sbuf("words_b%d" % s, [P, HALF], U16, tag=("q_bf", "q_raw")[s])
+            part = list_b[:, s * (HALF // 16) : (s + 1) * (HALF // 16)]
+            nc.vector.tensor_copy(words_b[:], pool_words[:].indirect(part))
+            b_bank = bank("b_bank%d" % s, 2 + s)
+            for h in range(2):
+                scores(b_bank[:, h * HALF : (h + 1) * HALF], h, words_b[:], scales_b[:, s * HALF : (s + 1) * HALF])
+            return b_bank
+
+        def vote(s, b_bank):
+            diff = sbuf("diff%d" % s, [P, 2, HALF], F32)
+            nc.vector.tensor_tensor(
+                diff[:],
+                a0[:, :, s * HALF : (s + 1) * HALF],
+                b_bank[:].rearrange("p (h i) -> p h i", h=2),
+                ALU.subtract,
+            )
+            nc.scalar.activation(votes[s][:], diff[:], ACT.Tanh)
+
+        def group_mean(s):
+            pair_bank = bank("pair_bank%d" % s, 4 + s)
+            for c in range(2):
+                for h in range(2):
+                    nc.tensor.matmul(
+                        pair_bank[:, c * P : (c + 1) * P],
+                        votes[s][:, h, c * P : (c + 1) * P],
+                        ident[:],
+                        start=(h == 0),
+                        stop=(h == 1),
+                        is_transpose=True,
+                    )
+            sums = sbuf("sums%d" % s, [P, 64], F32)
+            nc.vector.tensor_reduce(
+                sums[:], pair_bank[:, 0 : 2 * P].rearrange("p (c r) -> p c r", r=4), AXIS.X, ALU.add
+            )
+            means = sbuf("means%d" % s, [P, 64, 4], F32)
+            nc.vector.tensor_scalar(
+                means[:], sums[:].unsqueeze(2).to_broadcast([P, 64, 4]), 0.125, None, ALU.mult
+            )
+            flat = means[:].rearrange("p c r -> p (c r)")
+            for c in range(2):
+                col = (2 * s + c) * P
+                nc.tensor.transpose(vote_bank[:, col : col + P], flat[:, c * P : (c + 1) * P], ident[:])
+
+        b_banks = [opponents(s) for s in range(2)]
+        for s in range(2):
+            vote(s, b_banks[s])
+        gather_values(0)
+        gather_values(1)
+        for s in range(2):
+            group_mean(s)
+        quantize_values(0)
+        gather_values(2)
+        quantize_values(1)
+
+        probs = [sbuf("probs%d" % h, [P, PACK, P], F32, tag=("val_pool2", "probs1")[h]) for h in range(2)]
+        run_sums = [sbuf("run_sums%d" % h, [P, RUNS + 1], F32) for h in range(2)]
+
+        def softmax(h):
+            score = sbuf("score%d" % h, [P, I], F32)
+            nc.vector.scalar_tensor_tensor(
+                score[:], vote_bank[:], lam_cap[:, h, 0:1], a0[:, h, :], ALU.mult, ALU.add
+            )
+            neg_max = sbuf("neg_max%d" % h, [P, 1], F32)
+            nc.vector.tensor_reduce(neg_max[:], score[:], AXIS.X, ALU.max, negate=True)
+            nc.scalar.activation(
+                probs[h][:].rearrange("p t m -> p m t"),
+                score[:].rearrange("p (m t) -> p m t", t=PACK),
+                ACT.Exp,
+                bias=neg_max[:],
+                scale=1.0,
+                accum_out=run_sums[h][:, RUNS : RUNS + 1],
+            )
+
+
+        def turn_probs(h):
+            p_bank = bank("p_bank%d" % h, h)
+            for t in range(PACK):
+                nc.tensor.transpose(p_bank[:, t * P : (t + 1) * P], probs[h][:, t, :], ident[:])
+            for t in range(PACK):
+                nc.scalar.activation(
+                    scaled[h][:, t, :], p_bank[:, t * P : (t + 1) * P], ACT.Copy, scale=os_col[:, t : t + 1]
+                )
+
+        def factors(h):
+            nc.vector.tensor_reduce(
+                run_sums[h][:, 0:RUNS], probs[h][:].rearrange("p t (g a) -> p g t a", a=2), AXIS.XY, ALU.add
+            )
+            inverse = sbuf("inverse%d" % h, [P, RUNS + 1], F32)
+            nc.vector.reciprocal(inverse[:], run_sums[h][:])
+            factor = sbuf("factor%d" % h, [P, RUNS, 2], F32)
+            nc.vector.tensor_scalar(
+                factor[:],
+                inverse[:, 0:RUNS].unsqueeze(2).to_broadcast([P, RUNS, 2]),
+                lam_cap[:, h, 1:2],
+                inverse[:, RUNS : RUNS + 1],
+                ALU.mult,
+                ALU.min,
+            )
+            f_bank = bank("f_bank%d" % h, 2 + h)
+            nc.tensor.transpose(f_bank[:, 0:P], factor[:].rearrange("p g a -> p (g a)"), ident[:])
+            return f_bank
+
+        result = sbuf("result", [P, PACK, Q], F32)
+        result_bf = sbuf("result_bf", [P, Q, PACK], BF16)
+
+        def weights(h, f_bank):
+            w_bf = sbuf("w_bf%d" % h, [P, P, PACK], BF16)
+            nc.vector.tensor_tensor(
+                w_bf[:].rearrange("p (c i) t -> p c t i", i=2),
+                scaled[h][:].rearrange("p t (c i) -> p c t i", i=2),
+                f_bank[:, 0:P].rearrange("p (c i) -> p c i", i=2).unsqueeze(2).to_broadcast([P, P // 2, PACK, 2]),
+                ALU.mult,
+            )
+            w_codes = sbuf("w_codes%d" % h, [P, P], U32)
+            w_scales = sbuf("w_scales%d" % h, [P, P], U8)
+            nc.vector.quantize_mx(
+                out=w_codes[:].bitcast(FP8X4), scales=w_scales[:], in_=w_bf[:].rearrange("p m t -> p (m t)")
+            )
+            return w_codes, w_scales
+
+        def read(h, w_codes, w_scales):
+            o_bank = bank("o_bank%d" % h, 4 + h)
+            for j in range(PACK):
+                nc.tensor.matmul_mx(
+                    out=o_bank[:, j * P : (j + 1) * P],
+                    lhsT=v_codes[j][:].bitcast(FP8X4),
+                    lhsT_scale=v_scales[j][:],
+                    rhs=w_codes[:].bitcast(FP8X4),
+                    rhs_scale=w_scales[:],
+                    start=True,
+                    stop=True,
+                )
+            nc.scalar.copy(
+                result[:].rearrange("p j (v h r) -> p h j v r", h=2, r=4)[:, h],
+                o_bank[:].rearrange("p (j v r) -> p j v r", j=PACK, r=4),
+            )
+            nc.vector.tensor_copy(
+                result_bf[:].rearrange("p (v h r) j -> p h v j r", h=2, r=4)[:, h],
+                result[:].rearrange("p j (v h r) -> p h v j r", h=2, r=4)[:, h],
+            )
+
+        for h in range(2):
+            softmax(h)
+        quantize_values(2)
+        gather_values(3)
+        scaled = [sbuf("scaled%d" % h, [P, PACK, P], F32, tag=("val_pool3", "scaled1")[h]) for h in range(2)]
+        for h in range(2):
+            turn_probs(h)
+        f_banks = [factors(h) for h in range(2)]
+        quantize_values(3)
+        w_planes = [weights(h, f_banks[h]) for h in range(2)]
+        for h in range(2):
+            read(h, *w_planes[h])
+
+        nc.sync.dma_start(out_0.rearrange("(p j) q -> p j q", j=PACK), result[:])
+        o_codes = sbuf("o_codes", [P, Q], U32)
+        o_scales = sbuf("o_scales", [P, Q], U8)
+        nc.vector.quantize_mx(
+            out=o_codes[:].bitcast(FP8X4), scales=o_scales[:], in_=result_bf[:].rearrange("p q j -> p (q j)")
+        )
+        nc.sync.dma_start(out_1[0].rearrange("p q t -> p (q t)").bitcast(I32), o_codes[:].bitcast(I32))
+        for quad in range(4):
+            queue = nc.scalar if quad % 2 == 0 else nc.sync
+            queue.dma_start(
+                out_2[0][4 * quad : 4 * quad + 4, :].bitcast(I32),
+                o_scales[32 * quad : 32 * quad + 4, :].bitcast(I32),
+            )

@@ -56,166 +56,157 @@ def tile_attend_groupvotes_runcap_read_pl_kernel(
         nc.sync.dma_start(pool_words[:].bitcast(I32), keys_words[0].bitcast(I32))
         val_rows = vals.rearrange("(p j) t -> j p t", j=PACK)
         val_pool = [sbuf("val_pool%d" % j, [P, T], F32) for j in range(PACK)]
-        row_raw = sbuf("row_raw", [2, Q], F32)
+        rows = sbuf("rows", [P, Q], F32)
         os_col = sbuf("os_col", [P, PACK], F32)
-        nc.sync.dma_start(val_pool[0][:], val_rows[0])
-        nc.sync.dma_start(row_raw[0:1, :], lam)
-        nc.sync.dma_start(row_raw[1:2, :], cap.rearrange("q o -> o q"))
-        nc.sync.dma_start(os_col[:], slot_factor.rearrange("o (p t) -> (o p) t", t=PACK))
-        for j in range(1, PACK):
+        nc.gpsimd.memset(rows[:], 0.0)
+        nc.sync.dma_start(rows[0:1, :], lam)
+        nc.sync.dma_start(rows[1:2, :], cap.rearrange("q o -> o q"))
+        for j in range(PACK):
             nc.sync.dma_start(val_pool[j][:], val_rows[j])
+        nc.sync.dma_start(os_col[:], slot_factor.rearrange("o (p t) -> (o p) t", t=PACK))
 
         ident = sbuf("ident", [P, P], F32)
         make_identity(nc, ident[:])
-        row_dealt = sbuf("row_dealt", [P, Q], F32)
-        nc.gpsimd.memset(row_dealt[:], 0.0)
 
-        words_a = sbuf("words_a", [P, I], U16)
         scales_a = sbuf("scales_a", [P, I], U8)
         scales_b = sbuf("scales_b", [P, I], U8)
         nc.vector.tensor_copy(scales_a[:], pool_scales[:].indirect(list_a[:]))
         nc.vector.tensor_copy(scales_b[:], pool_scales[:].indirect(list_b[:]))
 
-        q_bf = sbuf("q_bf", [P, 2, P, PACK], BF16)
-        q_src = q_raw[:].rearrange("p j (v h r) -> p h v j r", h=2, r=4)
-        for h in range(2):
-            nc.scalar.copy(q_bf[:, h].rearrange("p (v r) j -> p v j r", r=4), q_src[:, h])
+        q_bf = sbuf("q_bf", [P, Q, PACK], BF16)
+        nc.scalar.copy(
+            q_bf[:].rearrange("p (c r) j -> p c j r", r=4), q_raw[:].rearrange("p j (c r) -> p c j r", r=4)
+        )
         q_codes = sbuf("q_codes", [P, Q], U32)
         q_scales = sbuf("q_scales", [P, Q], U8)
         nc.vector.quantize_mx(
-            out=q_codes[:].bitcast(FP8X4), scales=q_scales[:], in_=q_bf[:].rearrange("p h m j -> p (h m j)")
+            out=q_codes[:].bitcast(FP8X4), scales=q_scales[:], in_=q_bf[:].rearrange("p q j -> p (q j)")
         )
 
-        def scores(out, h, words, scales):
-            cols = slice(h * P, (h + 1) * P)
-            nc.tensor.matmul_mx(
-                out=out,
-                lhsT=q_codes[:, cols].bitcast(FP8X4),
-                lhsT_scale=q_scales[:, cols],
-                rhs=words.bitcast(FP4X4),
-                rhs_scale=scales,
-                start=True,
-                stop=True,
-            )
-
-        nc.vector.tensor_copy(words_a[:], pool_words[:].indirect(list_a[:]))
-        a0 = sbuf("a0", [P, 2, I], F32)
-        for s in range(2):
-            a_bank = bank("a_bank%d" % s, s)
-            slots = slice(s * HALF, (s + 1) * HALF)
-            for h in range(2):
-                scores(a_bank[:, h * HALF : (h + 1) * HALF], h, words_a[:, slots], scales_a[:, slots])
-            nc.scalar.copy(a0[:, :, slots], a_bank[:].rearrange("p (h i) -> p h i", h=2))
-
-        nc.gpsimd.tensor_copy(
-            row_dealt[0:2, :].rearrange("p (h v r) -> p h v r", h=2, r=4),
-            row_raw[:].rearrange("p (v h r) -> p h v r", h=2, r=4),
-        )
-        row_bank = bank("row_bank", 6)
+        col_bank = bank("col_bank", 7)
         for h in range(2):
-            nc.tensor.transpose(row_bank[:, h * P : (h + 1) * P], row_dealt[:, h * P : (h + 1) * P], ident[:])
+            nc.tensor.transpose(col_bank[:, h * P : (h + 1) * P], rows[:, h * P : (h + 1) * P], ident[:])
         lam_cap = sbuf("lam_cap", [P, 2, 2], F32)
-        nc.scalar.copy(lam_cap[:], row_bank[:, 0:Q].rearrange("p (h c) -> p h c", h=2)[:, :, 0:2])
+        nc.scalar.copy(lam_cap[:], col_bank[:, 0:Q].rearrange("p (h c) -> p h c", h=2)[:, :, 0:2])
+        lam_bank = bank("lam_bank", 6)
+        for h in range(2):
+            nc.tensor.transpose(lam_bank[:, h * P : (h + 1) * P], lam_cap[:, h, 0:1].to_broadcast([P, P]), ident[:])
+        lam_row = sbuf("lam_row", [P, Q], F32)
+        nc.scalar.activation(lam_row[:], lam_bank[:, 0:Q], ACT.Copy, scale=0.125)
 
-        v_codes = [sbuf("v_codes%d" % j, [P, P], U32) for j in range(PACK)]
-        v_scales = [sbuf("v_scales%d" % j, [P, P], U8) for j in range(PACK)]
-        v_bf = [sbuf("v_bf%d" % j, [P, P, PACK], BF16) for j in range(PACK)]
+        v_bf = []
+        v_planes = []
 
-        def gather_values(j):
-            picked = sbuf("picked%d" % j, [P, I], BF16, tag=("diff0", "diff1", "picked2", "picked3")[j])
-            if j == 0:
-                nc.vector.tensor_copy(picked[:], val_pool[j][:].indirect(list_a[:]))
-            else:
-                nc.scalar.activation(picked[:], val_pool[j][:].indirect(list_a[:]), ACT.Copy)
-            pairs = picked[:].bitcast(F32)
-            turned = bank("turned%d" % j, 7)
-            for u in range(2):
-                nc.tensor.transpose(turned[:, u * P : (u + 1) * P], pairs[:, u : I // 2 : 2], ident[:])
+        def gather_values(j, tag):
+            picked = sbuf("picked%d" % j, [P, I], BF16, tag=tag)
+            nc.scalar.activation(picked[:], val_pool[j][:].indirect(list_a[:]), ACT.Copy)
+            return picked
+
+        def turn_values(pair, picked, number, tag):
+            turned = bank("turned%d" % pair, number)
+            for j in range(2):
+                words = picked[j][:].bitcast(F32)
+                for u in range(2):
+                    col = (2 * j + u) * P
+                    nc.tensor.transpose(turned[:, col : col + P], words[:, u : I // 2 : 2], ident[:])
+            v_bf.append(sbuf("v_bf%d" % pair, [P, 2, P, PACK], BF16, tag=tag))
             nc.scalar.copy(
-                v_bf[j][:].rearrange("p m t -> p (m t)").bitcast(F32).rearrange("p (m u) -> p m u", u=2),
-                turned[:, 0 : 2 * P].rearrange("p (u m) -> p m u", u=2),
+                v_bf[pair][:].rearrange("p j m t -> p (j m t)").bitcast(F32).rearrange("p (j m u) -> p j m u", j=2, u=2),
+                turned[:].rearrange("p (j u m) -> p j m u", j=2, u=2),
             )
 
-        def quantize_values(j):
+        def quantize_values(pair, tag):
+            codes = sbuf("v_codes%d" % pair, [P, 2 * P], U32, tag=tag)
+            scales = sbuf("v_scales%d" % pair, [P, 2 * P], U8)
             nc.vector.quantize_mx(
-                out=v_codes[j][:].bitcast(FP8X4), scales=v_scales[j][:], in_=v_bf[j][:].rearrange("p m t -> p (m t)")
+                out=codes[:].bitcast(FP8X4), scales=scales[:], in_=v_bf[pair][:].rearrange("p j m t -> p (j m t)")
             )
+            v_planes.append((codes, scales))
 
-        votes = [sbuf("votes%d" % s, [P, 2, HALF], F32) for s in range(2)]
-        vote_bank = bank("vote_bank", 6)
-
-        def opponents(s):
-            words_b = sbuf("words_b%d" % s, [P, HALF], U16, tag=("q_bf", "q_raw")[s])
-            part = list_b[:, s * (HALF // 16) : (s + 1) * (HALF // 16)]
-            nc.vector.tensor_copy(words_b[:], pool_words[:].indirect(part))
-            b_bank = bank("b_bank%d" % s, 2 + s)
-            for h in range(2):
-                scores(b_bank[:, h * HALF : (h + 1) * HALF], h, words_b[:], scales_b[:, s * HALF : (s + 1) * HALF])
-            return b_bank
-
-        def vote(s, b_bank):
-            diff = sbuf("diff%d" % s, [P, 2, HALF], F32)
-            nc.vector.tensor_tensor(
-                diff[:],
-                a0[:, :, s * HALF : (s + 1) * HALF],
-                b_bank[:].rearrange("p (h i) -> p h i", h=2),
-                ALU.subtract,
-            )
-            nc.scalar.activation(votes[s][:], diff[:], ACT.Tanh)
-
-        def group_mean(s):
-            pair_bank = bank("pair_bank%d" % s, 4 + s)
+        def products(name, s, offsets, scales, number, tag):
+            words = sbuf("words_%s%d" % (name, s), [P, HALF], U16, tag=tag)
+            part = offsets[:, s * (HALF // 16) : (s + 1) * (HALF // 16)]
+            nc.vector.tensor_copy(words[:], pool_words[:].indirect(part))
+            sums = bank("%s_bank%d" % (name, s), number)
             for c in range(2):
-                for h in range(2):
+                first = s * HALF + c * P
+                nc.tensor.matmul_mx(
+                    out=sums[:, c * Q : (c + 1) * Q],
+                    lhsT=words[:, c * P : (c + 1) * P].bitcast(FP4X4),
+                    lhsT_scale=scales[:, first : first + P],
+                    rhs=q_codes[:].bitcast(FP8X4),
+                    rhs_scale=q_scales[:],
+                    start=True,
+                    stop=True,
+                )
+            return sums
+
+        a0 = []
+        picked = []
+        b_banks = []
+        for s in range(2):
+            a_bank = products("a", s, list_a, scales_a, s, (None, "q_raw")[s])
+            a0.append(sbuf("a0_%d" % s, [P, BANK], F32, tag=(None, "val_pool0")[s]))
+            nc.scalar.copy(a0[s][:], a_bank[:])
+            if s == 0:
+                picked.append(gather_values(0, "words_a0"))
+            b_banks.append(products("b", s, list_b, scales_b, 2 + s, ("q_bf", None)[s]))
+
+        score = [bank("score%d" % h, 4 + h) for h in range(2)]
+
+        def turn_into_scores(src, s, first, last):
+            for h in range(2):
+                for c in range(2):
+                    col = s * HALF + c * P
                     nc.tensor.matmul(
-                        pair_bank[:, c * P : (c + 1) * P],
-                        votes[s][:, h, c * P : (c + 1) * P],
+                        score[h][:, col : col + P],
+                        src[:, c * Q + h * P : c * Q + (h + 1) * P],
                         ident[:],
-                        start=(h == 0),
-                        stop=(h == 1),
+                        start=(first and c == 0),
+                        stop=(last and c == 1),
                         is_transpose=True,
                     )
+
+        def vote(s):
+            diff = sbuf("diff%d" % s, [P, BANK], F32)
+            nc.vector.tensor_tensor(diff[:], a0[s][:], b_banks[s][:], ALU.subtract)
+            votes = sbuf("votes%d" % s, [P, BANK], F32)
+            nc.scalar.activation(votes[:], diff[:], ACT.Tanh)
+            return votes
+
+        def weigh_votes(s, votes):
             sums = sbuf("sums%d" % s, [P, 64], F32)
-            nc.vector.tensor_reduce(
-                sums[:], pair_bank[:, 0 : 2 * P].rearrange("p (c r) -> p c r", r=4), AXIS.X, ALU.add
+            nc.vector.tensor_reduce(sums[:], votes[:].rearrange("p (c r) -> p c r", r=8), AXIS.X, ALU.add)
+            bonus = sbuf("bonus%d" % s, [P, 2, 32, 8], F32)
+            nc.vector.tensor_tensor(
+                bonus[:],
+                sums[:].rearrange("p (c v) -> p c v", c=2).unsqueeze(3).to_broadcast([P, 2, 32, 8]),
+                lam_row[:].rearrange("p (v r) -> p v r", r=8).unsqueeze(1).to_broadcast([P, 2, 32, 8]),
+                ALU.mult,
             )
-            means = sbuf("means%d" % s, [P, 64, 4], F32)
-            nc.vector.tensor_scalar(
-                means[:], sums[:].unsqueeze(2).to_broadcast([P, 64, 4]), 0.125, None, ALU.mult
-            )
-            flat = means[:].rearrange("p c r -> p (c r)")
-            for c in range(2):
-                col = (2 * s + c) * P
-                nc.tensor.transpose(vote_bank[:, col : col + P], flat[:, c * P : (c + 1) * P], ident[:])
+            turn_into_scores(bonus[:].rearrange("p c v r -> p (c v r)"), s, False, s == 1)
 
-        b_banks = [opponents(s) for s in range(2)]
+        votes = [vote(s) for s in range(2)]
         for s in range(2):
-            vote(s, b_banks[s])
-        gather_values(0)
-        gather_values(1)
+            turn_into_scores(a0[s][:], s, s == 0, False)
+        picked += [gather_values(1, "diff1"), gather_values(2, "val_pool1")]
         for s in range(2):
-            group_mean(s)
-        quantize_values(0)
-        gather_values(2)
-        quantize_values(1)
+            weigh_votes(s, votes[s])
 
-        probs = [sbuf("probs%d" % h, [P, PACK, P], F32, tag=("val_pool2", "probs1")[h]) for h in range(2)]
-        run_sums = [sbuf("run_sums%d" % h, [P, RUNS + 1], F32) for h in range(2)]
+        probs = []
+        totals = [sbuf("total%d" % h, [P, 1], F32) for h in range(2)]
 
         def softmax(h):
-            score = sbuf("score%d" % h, [P, I], F32)
-            nc.vector.scalar_tensor_tensor(
-                score[:], vote_bank[:], lam_cap[:, h, 0:1], a0[:, h, :], ALU.mult, ALU.add
-            )
             neg_max = sbuf("neg_max%d" % h, [P, 1], F32)
-            nc.vector.tensor_reduce(neg_max[:], score[:], AXIS.X, ALU.max, negate=True)
+            nc.vector.tensor_reduce(neg_max[:], score[h][:], AXIS.X, ALU.max, negate=True)
+            probs.append(sbuf("probs%d" % h, [P, PACK, P], F32, tag=("val_pool2", "probs1")[h]))
             nc.scalar.activation(
                 probs[h][:].rearrange("p t m -> p m t"),
-                score[:].rearrange("p (m t) -> p m t", t=PACK),
+                score[h][:].rearrange("p (m t) -> p m t", t=PACK),
                 ACT.Exp,
                 bias=neg_max[:],
                 scale=1.0,
-                accum_out=run_sums[h][:, RUNS : RUNS + 1],
+                accum_out=totals[h][:],
             )
 
 
@@ -229,26 +220,26 @@ def tile_attend_groupvotes_runcap_read_pl_kernel(
                 )
 
         def factors(h):
+            run_sums = sbuf("run_sums%d" % h, [P, RUNS], F32, tag=(None, "inverse0")[h])
             nc.vector.tensor_reduce(
-                run_sums[h][:, 0:RUNS], probs[h][:].rearrange("p t (g a) -> p g t a", a=2), AXIS.XY, ALU.add
+                run_sums[:], probs[h][:].rearrange("p t (g a) -> p g t a", a=2), AXIS.XY, ALU.add
             )
-            inverse = sbuf("inverse%d" % h, [P, RUNS + 1], F32)
-            nc.vector.reciprocal(inverse[:], run_sums[h][:])
+            inverse_total = sbuf("inverse_total%d" % h, [P, 1], F32)
+            nc.vector.reciprocal(inverse_total[:], totals[h][:])
+            inverse = sbuf("inverse%d" % h, [P, RUNS], F32)
+            nc.vector.reciprocal(inverse[:], run_sums[:])
             factor = sbuf("factor%d" % h, [P, RUNS, 2], F32)
             nc.vector.tensor_scalar(
                 factor[:],
-                inverse[:, 0:RUNS].unsqueeze(2).to_broadcast([P, RUNS, 2]),
+                inverse[:].unsqueeze(2).to_broadcast([P, RUNS, 2]),
                 lam_cap[:, h, 1:2],
-                inverse[:, RUNS : RUNS + 1],
+                inverse_total[:],
                 ALU.mult,
                 ALU.min,
             )
             f_bank = bank("f_bank%d" % h, 2 + h)
             nc.tensor.transpose(f_bank[:, 0:P], factor[:].rearrange("p g a -> p (g a)"), ident[:])
             return f_bank
-
-        result = sbuf("result", [P, PACK, Q], F32)
-        result_bf = sbuf("result_bf", [P, Q, PACK], BF16)
 
         def weights(h, f_bank):
             w_bf = sbuf("w_bf%d" % h, [P, P, PACK], BF16)
@@ -258,6 +249,9 @@ def tile_attend_groupvotes_runcap_read_pl_kernel(
                 f_bank[:, 0:P].rearrange("p (c i) -> p c i", i=2).unsqueeze(2).to_broadcast([P, P // 2, PACK, 2]),
                 ALU.mult,
             )
+            return w_bf
+
+        def quantize_weights(h, w_bf):
             w_codes = sbuf("w_codes%d" % h, [P, P], U32)
             w_scales = sbuf("w_scales%d" % h, [P, P], U8)
             nc.vector.quantize_mx(
@@ -270,42 +264,48 @@ def tile_attend_groupvotes_runcap_read_pl_kernel(
             for j in range(PACK):
                 nc.tensor.matmul_mx(
                     out=o_bank[:, j * P : (j + 1) * P],
-                    lhsT=v_codes[j][:].bitcast(FP8X4),
-                    lhsT_scale=v_scales[j][:],
+                    lhsT=v_planes[j // 2][0][:, (j % 2) * P : (j % 2 + 1) * P].bitcast(FP8X4),
+                    lhsT_scale=v_planes[j // 2][1][:, (j % 2) * P : (j % 2 + 1) * P],
                     rhs=w_codes[:].bitcast(FP8X4),
                     rhs_scale=w_scales[:],
                     start=True,
                     stop=True,
                 )
-            nc.scalar.copy(
-                result[:].rearrange("p j (v h r) -> p h j v r", h=2, r=4)[:, h],
-                o_bank[:].rearrange("p (j v r) -> p j v r", j=PACK, r=4),
-            )
+            cols = slice(h * P, (h + 1) * P)
+            result = sbuf("result%d" % h, [P, PACK, P], F32)
+            nc.scalar.copy(result[:].rearrange("p j q -> p (j q)"), o_bank[:])
+            nc.sync.dma_start(out_0.rearrange("(p j) q -> p j q", j=PACK)[:, :, cols], result[:])
+            result_bf = sbuf("result_bf%d" % h, [P, P, PACK], BF16)
             nc.vector.tensor_copy(
-                result_bf[:].rearrange("p (v h r) j -> p h v j r", h=2, r=4)[:, h],
-                result[:].rearrange("p j (v h r) -> p h v j r", h=2, r=4)[:, h],
+                result_bf[:].rearrange("p (c r) j -> p c j r", r=4), result[:].rearrange("p j (c r) -> p c j r", r=4)
+            )
+            o_codes = sbuf("o_codes%d" % h, [P, P], U32)
+            nc.vector.quantize_mx(
+                out=o_codes[:].bitcast(FP8X4), scales=o_scales[:, cols], in_=result_bf[:].rearrange("p q j -> p (q j)")
+            )
+            nc.sync.dma_start(
+                out_1[0].rearrange("p q t -> p (q t)").bitcast(I32)[:, cols], o_codes[:].bitcast(I32)
             )
 
-        for h in range(2):
-            softmax(h)
-        quantize_values(2)
-        gather_values(3)
+        o_scales = sbuf("o_scales", [P, Q], U8)
+        softmax(0)
+        turn_values(0, picked[0:2], 6, "neg_max0")
+        softmax(1)
+        picked.append(gather_values(3, "neg_max1"))
         scaled = [sbuf("scaled%d" % h, [P, PACK, P], F32, tag=("val_pool3", "scaled1")[h]) for h in range(2)]
-        for h in range(2):
-            turn_probs(h)
-        f_banks = [factors(h) for h in range(2)]
-        quantize_values(3)
-        w_planes = [weights(h, f_banks[h]) for h in range(2)]
+        turn_probs(0)
+        turn_values(1, picked[2:4], 7, None)
+        turn_probs(1)
+        f_bank0 = factors(0)
+        quantize_values(0, "inverse_total0")
+        f_bank1 = factors(1)
+        w_bf0 = weights(0, f_bank0)
+        quantize_values(1, "val_pool3")
+        planes0 = quantize_weights(0, w_bf0)
+        w_planes = [planes0, quantize_weights(1, weights(1, f_bank1))]
         for h in range(2):
             read(h, *w_planes[h])
 
-        nc.sync.dma_start(out_0.rearrange("(p j) q -> p j q", j=PACK), result[:])
-        o_codes = sbuf("o_codes", [P, Q], U32)
-        o_scales = sbuf("o_scales", [P, Q], U8)
-        nc.vector.quantize_mx(
-            out=o_codes[:].bitcast(FP8X4), scales=o_scales[:], in_=result_bf[:].rearrange("p q j -> p (q j)")
-        )
-        nc.sync.dma_start(out_1[0].rearrange("p q t -> p (q t)").bitcast(I32), o_codes[:].bitcast(I32))
         for quad in range(4):
             queue = nc.scalar if quad % 2 == 0 else nc.sync
             queue.dma_start(

@@ -152,7 +152,7 @@ def tile_attend_groupvotes_runcap_read_pl_kernel(
                 picked.append(gather_values(0, "words_a0"))
             b_banks.append(products("b", s, list_b, scales_b, 2 + s, ("q_bf", None)[s]))
 
-        score = [bank("score%d" % h, 4 + h) for h in range(2)]
+        score = []
 
         def turn_into_scores(src, s, first, last):
             for h in range(2):
@@ -170,7 +170,7 @@ def tile_attend_groupvotes_runcap_read_pl_kernel(
         def vote(s):
             diff = sbuf("diff%d" % s, [P, BANK], F32)
             nc.vector.tensor_tensor(diff[:], a0[s][:], b_banks[s][:], ALU.subtract)
-            votes = sbuf("votes%d" % s, [P, BANK], F32)
+            votes = sbuf("votes%d" % s, [P, BANK], F32, tag=("q_raw", None)[s])
             nc.scalar.activation(votes[:], diff[:], ACT.Tanh)
             return votes
 
@@ -187,6 +187,7 @@ def tile_attend_groupvotes_runcap_read_pl_kernel(
             turn_into_scores(bonus[:].rearrange("p c v r -> p (c v r)"), s, False, s == 1)
 
         votes = [vote(s) for s in range(2)]
+        score += [bank("score%d" % h, 3 - h) for h in range(2)]
         for s in range(2):
             turn_into_scores(a0[s][:], s, s == 0, False)
         picked += [gather_values(1, "diff1"), gather_values(2, "val_pool1")]
@@ -201,8 +202,8 @@ def tile_attend_groupvotes_runcap_read_pl_kernel(
             nc.vector.tensor_reduce(neg_max[:], score[h][:], AXIS.X, ALU.max, negate=True)
             probs.append(sbuf("probs%d" % h, [P, PACK, P], F32, tag=("val_pool2", "probs1")[h]))
             nc.scalar.activation(
-                probs[h][:].rearrange("p t m -> p m t"),
-                score[h][:].rearrange("p (m t) -> p m t", t=PACK),
+                probs[h][:],
+                score[h][:].rearrange("p (m t) -> p t m", t=PACK),
                 ACT.Exp,
                 bias=neg_max[:],
                 scale=1.0,
@@ -211,7 +212,7 @@ def tile_attend_groupvotes_runcap_read_pl_kernel(
 
 
         def turn_probs(h):
-            p_bank = bank("p_bank%d" % h, h)
+            p_bank = bank("p_bank%d" % h, (0, 6)[h])
             for t in range(PACK):
                 nc.tensor.transpose(p_bank[:, t * P : (t + 1) * P], probs[h][:, t, :], ident[:])
             for t in range(PACK):
@@ -237,12 +238,12 @@ def tile_attend_groupvotes_runcap_read_pl_kernel(
                 ALU.mult,
                 ALU.min,
             )
-            f_bank = bank("f_bank%d" % h, 2 + h)
+            f_bank = bank("f_bank%d" % h, 4 + h)
             nc.tensor.transpose(f_bank[:, 0:P], factor[:].rearrange("p g a -> p (g a)"), ident[:])
             return f_bank
 
         def weights(h, f_bank):
-            w_bf = sbuf("w_bf%d" % h, [P, P, PACK], BF16)
+            w_bf = sbuf("w_bf%d" % h, [P, P, PACK], BF16, tag=("inverse1", None)[h])
             nc.vector.tensor_tensor(
                 w_bf[:].rearrange("p (c i) t -> p c t i", i=2),
                 scaled[h][:].rearrange("p t (c i) -> p c t i", i=2),
@@ -260,7 +261,7 @@ def tile_attend_groupvotes_runcap_read_pl_kernel(
             return w_codes, w_scales
 
         def read(h, w_codes, w_scales):
-            o_bank = bank("o_bank%d" % h, 4 + h)
+            o_bank = bank("o_bank%d" % h, 3 - h)
             for j in range(PACK):
                 nc.tensor.matmul_mx(
                     out=o_bank[:, j * P : (j + 1) * P],
@@ -289,7 +290,7 @@ def tile_attend_groupvotes_runcap_read_pl_kernel(
 
         o_scales = sbuf("o_scales", [P, Q], U8)
         softmax(0)
-        turn_values(0, picked[0:2], 6, "neg_max0")
+        turn_values(0, picked[0:2], 1, "neg_max0")
         softmax(1)
         picked.append(gather_values(3, "neg_max1"))
         scaled = [sbuf("scaled%d" % h, [P, PACK, P], F32, tag=("val_pool3", "scaled1")[h]) for h in range(2)]

from contextlib import ExitStack

import concourse.mybir as mybir
from concourse.masks import make_identity

D, T, I, Q, E = 512, 2048, 512, 256, 512
FLOPS = 3 * 2 * 512 * 512 * 256

F32 = mybir.dt.float32
BF16 = mybir.dt.bfloat16
I32 = mybir.dt.int32
U32 = mybir.dt.uint32
U16 = mybir.dt.uint16
U8 = mybir.dt.uint8
FP8X4 = mybir.dt.float8_e4m3fn_x4
FP4X4 = mybir.dt.float4_e2m1fn_x4
ALU = mybir.AluOpType
ACT = mybir.ActivationFunctionType
AXIS = mybir.AxisListType

P = 128
PACK = 4
BANK = 512
HALF = I // 2
RUNS = 64


def tile_attend_groupvotes_runcap_read_pl_kernel(
    tc, query, keys_words, keys_scales, lam, cap, slot_factor, vals, offs, offs2, out_0, out_1, out_2
):
    nc = tc.nc
    with ExitStack() as ctx:
        sb = ctx.enter_context(tc.tile_pool(name="sb", bufs=1))
        ps = ctx.enter_context(tc.psum_pool(name="ps", bufs=1))

        def sbuf(name, shape, dtype, tag=None):
            return sb.tile(shape, dtype, name=name, tag=tag or name, align_bytes=64)

        def bank(name, number):
            return ps.tile([P, BANK], F32, name=name, tag="bank%d" % number)

        list_a = sb.tile([P, I // 16], U16, name="list_a")
        list_b = sb.tile([P, I // 16], U16, name="list_b")
        pool_words = sbuf("pool_words", [P, T], U16)
        pool_scales = sbuf("pool_scales", [P, T], U8)
        q_raw = sbuf("q_raw", [P, PACK, Q], F32)
        nc.gpsimd.memset(pool_scales[:].bitcast(I32), 0)
        nc.sync.dma_start(list_a[:], offs)
        nc.sync.dma_start(list_b[:], offs2)
        for quad in range(4):
            nc.sync.dma_start(
                pool_scales[32 * quad : 32 * quad + 4, :].bitcast(I32),
                keys_scales[0][4 * quad : 4 * quad + 4, :].bitcast(I32),
            )
        nc.sync.dma_start(q_raw[:], query.rearrange("(p j) q -> p j q", j=PACK))
        nc.sync.dma_start(pool_words[:].bitcast(I32), keys_words[0].bitcast(I32))
        val_rows = vals.rearrange("(p j) t -> j p t", j=PACK)
        val_pool = [sbuf("val_pool%d" % j, [P, T], F32) for j in range(PACK)]
        rows = sbuf("rows", [P, Q], F32)
        os_col = sbuf("os_col", [P, PACK], F32)
        nc.gpsimd.memset(rows[:], 0.0)
        nc.sync.dma_start(rows[0:1, :], lam)
        nc.sync.dma_start(rows[1:2, :], cap.rearrange("q o -> o q"))
        for j in range(PACK):
            nc.sync.dma_start(val_pool[j][:], val_rows[j])
        nc.sync.dma_start(os_col[:], slot_factor.rearrange("o (p t) -> (o p) t", t=PACK))

        ident = sbuf("ident", [P, P], F32)
        make_identity(nc, ident[:])

        scales_a = sbuf("scales_a", [P, I], U8)
        scales_b = sbuf("scales_b", [P, I], U8)
        nc.vector.tensor_copy(scales_a[:], pool_scales[:].indirect(list_a[:]))
        nc.vector.tensor_copy(scales_b[:], pool_scales[:].indirect(list_b[:]))

        q_bf = sbuf("q_bf", [P, Q, PACK], BF16)
        nc.scalar.copy(
            q_bf[:].rearrange("p (c r) j -> p c j r", r=4), q_raw[:].rearrange("p j (c r) -> p c j r", r=4)
        )
        q_codes = sbuf("q_codes", [P, Q], U32)
        q_scales = sbuf("q_scales", [P, Q], U8)
        nc.vector.quantize_mx(
            out=q_codes[:].bitcast(FP8X4), scales=q_scales[:], in_=q_bf[:].rearrange("p q j -> p (q j)")
        )

        col_bank = bank("col_bank", 7)
        for h in range(2):
            nc.tensor.transpose(col_bank[:, h * P : (h + 1) * P], rows[:, h * P : (h + 1) * P], ident[:])
        lam_cap = sbuf("lam_cap", [P, 2, 2], F32)
        nc.scalar.copy(lam_cap[:], col_bank[:, 0:Q].rearrange("p (h c) -> p h c", h=2)[:, :, 0:2])
        lam_bank = bank("lam_bank", 6)
        for h in range(2):
            nc.tensor.transpose(lam_bank[:, h * P : (h + 1) * P], lam_cap[:, h, 0:1].to_broadcast([P, P]), ident[:])
        lam_row = sbuf("lam_row", [P, Q], F32)
        nc.scalar.activation(lam_row[:], lam_bank[:, 0:Q], ACT.Copy, scale=0.125)

        v_bf = []
        v_planes = []

        def gather_values(j, tag):
            picked = sbuf("picked%d" % j, [P, I], BF16, tag=tag)
            nc.scalar.activation(picked[:], val_pool[j][:].indirect(list_a[:]), ACT.Copy)
            return picked

        def turn_values(pair, picked, number, tag):
            turned = bank("turned%d" % pair, number)
            for j in range(2):
                words = picked[j][:].bitcast(F32)
                for u in range(2):
                    col = (2 * j + u) * P
                    nc.tensor.transpose(turned[:, col : col + P], words[:, u : I // 2 : 2], ident[:])
            v_bf.append(sbuf("v_bf%d" % pair, [P, 2, P, PACK], BF16, tag=tag))
            nc.scalar.copy(
                v_bf[pair][:].rearrange("p j m t -> p (j m t)").bitcast(F32).rearrange("p (j m u) -> p j m u", j=2, u=2),
                turned[:].rearrange("p (j u m) -> p j m u", j=2, u=2),
            )

        def quantize_values(pair, tag):
            codes = sbuf("v_codes%d" % pair, [P, 2 * P], U32, tag=tag)
            scales = sbuf("v_scales%d" % pair, [P, 2 * P], U8)
            nc.vector.quantize_mx(
                out=codes[:].bitcast(FP8X4), scales=scales[:], in_=v_bf[pair][:].rearrange("p j m t -> p (j m t)")
            )
            v_planes.append((codes, scales))

        def products(name, s, offsets, scales, number, tag):
            words = sbuf("words_%s%d" % (name, s), [P, HALF], U16, tag=tag)
            part = offsets[:, s * (HALF // 16) : (s + 1) * (HALF // 16)]
            nc.vector.tensor_copy(words[:], pool_words[:].indirect(part))
            sums = bank("%s_bank%d" % (name, s), number)
            for c in range(2):
                first = s * HALF + c * P
                nc.tensor.matmul_mx(
                    out=sums[:, c * Q : (c + 1) * Q],
                    lhsT=words[:, c * P : (c + 1) * P].bitcast(FP4X4),
                    lhsT_scale=scales[:, first : first + P],
                    rhs=q_codes[:].bitcast(FP8X4),
                    rhs_scale=q_scales[:],
                    start=True,
                    stop=True,
                )
            return sums

        a0 = []
        picked = []
        b_banks = []
        for s in range(2):
            a_bank = products("a", s, list_a, scales_a, s, (None, "q_raw")[s])
            a0.append(sbuf("a0_%d" % s, [P, BANK], F32, tag=(None, "val_pool0")[s]))
            nc.scalar.copy(a0[s][:], a_bank[:])
            if s == 0:
                picked.append(gather_values(0, "words_a0"))
            b_banks.append(products("b", s, list_b, scales_b, 2 + s, ("q_bf", None)[s]))

        score = []

        def turn_into_scores(src, s, first, last):
            for h in range(2):
                for c in range(2):
                    col = s * HALF + c * P
                    nc.tensor.matmul(
                        score[h][:, col : col + P],
                        src[:, c * Q + h * P : c * Q + (h + 1) * P],
                        ident[:],
                        start=(first and c == 0),
                        stop=(last and c == 1),
                        is_transpose=True,
                    )

        def vote(s):
            diff = sbuf("diff%d" % s, [P, BANK], F32)
            nc.vector.tensor_tensor(diff[:], a0[s][:], b_banks[s][:], ALU.subtract)
            votes = sbuf("votes%d" % s, [P, BANK], F32, tag=("q_raw", None)[s])
            nc.scalar.activation(votes[:], diff[:], ACT.Tanh)
            return votes

        def weigh_votes(s, votes):
            sums = sbuf("sums%d" % s, [P, 64], F32)
            nc.vector.tensor_reduce(sums[:], votes[:].rearrange("p (c r) -> p c r", r=8), AXIS.X, ALU.add)
            bonus = sbuf("bonus%d" % s, [P, 2, 32, 8], F32)
            nc.vector.tensor_tensor(
                bonus[:],
                sums[:].rearrange("p (c v) -> p c v", c=2).unsqueeze(3).to_broadcast([P, 2, 32, 8]),
                lam_row[:].rearrange("p (v r) -> p v r", r=8).unsqueeze(1).to_broadcast([P, 2, 32, 8]),
                ALU.mult,
            )
            turn_into_scores(bonus[:].rearrange("p c v r -> p (c v r)"), s, False, s == 1)

        votes = [vote(s) for s in range(2)]
        score += [bank("score%d" % h, 3 - h) for h in range(2)]
        for s in range(2):
            turn_into_scores(a0[s][:], s, s == 0, False)
        picked += [gather_values(1, "diff1"), gather_values(2, "val_pool1")]
        for s in range(2):
            weigh_votes(s, votes[s])

        probs = []
        totals = [sbuf("total%d" % h, [P, 1], F32) for h in range(2)]

        def softmax(h):
            neg_max = sbuf("neg_max%d" % h, [P, 1], F32)
            nc.vector.tensor_reduce(neg_max[:], score[h][:], AXIS.X, ALU.max, negate=True)
            probs.append(sbuf("probs%d" % h, [P, PACK, P], F32, tag=("val_pool2", "probs1")[h]))
            nc.scalar.activation(
                probs[h][:],
                score[h][:].rearrange("p (m t) -> p t m", t=PACK),
                ACT.Exp,
                bias=neg_max[:],
                scale=1.0,
                accum_out=totals[h][:],
            )


        def turn_probs(h):
            p_bank = bank("p_bank%d" % h, (0, 6)[h])
            for t in range(PACK):
                nc.tensor.transpose(p_bank[:, t * P : (t + 1) * P], probs[h][:, t, :], ident[:])
            for t in range(PACK):
                nc.scalar.activation(
                    scaled[h][:, t, :], p_bank[:, t * P : (t + 1) * P], ACT.Copy, scale=os_col[:, t : t + 1]
                )

        def factors(h):
            run_sums = sbuf("run_sums%d" % h, [P, RUNS], F32, tag=(None, "inverse0")[h])
            nc.vector.tensor_reduce(
                run_sums[:], probs[h][:].rearrange("p t (g a) -> p g t a", a=2), AXIS.XY, ALU.add
            )
            inverse_total = sbuf("inverse_total%d" % h, [P, 1], F32)
            nc.vector.reciprocal(inverse_total[:], totals[h][:])
            inverse = sbuf("inverse%d" % h, [P, RUNS], F32)
            nc.vector.reciprocal(inverse[:], run_sums[:])
            factor = sbuf("factor%d" % h, [P, RUNS, 2], F32)
            nc.vector.tensor_scalar(
                factor[:],
                inverse[:].unsqueeze(2).to_broadcast([P, RUNS, 2]),
                lam_cap[:, h, 1:2],
                inverse_total[:],
                ALU.mult,
                ALU.min,
            )
            f_bank = bank("f_bank%d" % h, 4 + h)
            nc.tensor.transpose(f_bank[:, 0:P], factor[:].rearrange("p g a -> p (g a)"), ident[:])
            return f_bank

        def weights(h, f_bank):
            w_bf = sbuf("w_bf%d" % h, [P, P, PACK], BF16, tag=("inverse1", None)[h])
            nc.vector.tensor_tensor(
                w_bf[:].rearrange("p (c i) t -> p c t i", i=2),
                scaled[h][:].rearrange("p t (c i) -> p c t i", i=2),
                f_bank[:, 0:P].rearrange("p (c i) -> p c i", i=2).unsqueeze(2).to_broadcast([P, P // 2, PACK, 2]),
                ALU.mult,
            )
            return w_bf

        def quantize_weights(h, w_bf):
            w_codes = sbuf("w_codes%d" % h, [P, P], U32)
            w_scales = sbuf("w_scales%d" % h, [P, P], U8)
            nc.vector.quantize_mx(
                out=w_codes[:].bitcast(FP8X4), scales=w_scales[:], in_=w_bf[:].rearrange("p m t -> p (m t)")
            )
            return w_codes, w_scales

        def read(h, w_codes, w_scales):
            o_bank = bank("o_bank%d" % h, 3 - h)
            for j in range(PACK):
                nc.tensor.matmul_mx(
                    out=o_bank[:, j * P : (j + 1) * P],
                    lhsT=v_planes[j // 2][0][:, (j % 2) * P : (j % 2 + 1) * P].bitcast(FP8X4),
                    lhsT_scale=v_planes[j // 2][1][:, (j % 2) * P : (j % 2 + 1) * P],
                    rhs=w_codes[:].bitcast(FP8X4),
                    rhs_scale=w_scales[:],
                    start=True,
                    stop=True,
                )
            cols = slice(h * P, (h + 1) * P)
            result = sbuf("result%d" % h, [P, PACK, P], F32)
            nc.scalar.copy(result[:].rearrange("p j q -> p (j q)"), o_bank[:])
            nc.sync.dma_start(out_0.rearrange("(p j) q -> p j q", j=PACK)[:, :, cols], result[:])
            result_bf = sbuf("result_bf%d" % h, [P, P, PACK], BF16)
            nc.vector.tensor_copy(
                result_bf[:].rearrange("p (c r) j -> p c j r", r=4), result[:].rearrange("p j (c r) -> p c j r", r=4)
            )
            o_codes = sbuf("o_codes%d" % h, [P, P], U32)
            nc.vector.quantize_mx(
                out=o_codes[:].bitcast(FP8X4), scales=o_scales[:, cols], in_=result_bf[:].rearrange("p q j -> p (q j)")
            )
            nc.sync.dma_start(
                out_1[0].rearrange("p q t -> p (q t)").bitcast(I32)[:, cols], o_codes[:].bitcast(I32)
            )

        o_scales = sbuf("o_scales", [P, Q], U8)
        softmax(0)
        turn_values(0, picked[0:2], 1, "neg_max0")
        softmax(1)
        picked.append(gather_values(3, "neg_max1"))
        scaled = [sbuf("scaled%d" % h, [P, PACK, P], F32, tag=("val_pool3", "scaled1")[h]) for h in range(2)]
        turn_probs(0)
        turn_values(1, picked[2:4], 7, None)
        turn_probs(1)
        f_bank0 = factors(0)
        quantize_values(0, "inverse_total0")
        f_bank1 = factors(1)
        w_bf0 = weights(0, f_bank0)
        quantize_values(1, "val_pool3")
        planes0 = quantize_weights(0, w_bf0)
        w_planes = [planes0, quantize_weights(1, weights(1, f_bank1))]
        for h in range(2):
            read(h, *w_planes[h])

        for quad in range(4):
            queue = nc.scalar if quad % 2 == 0 else nc.sync
            queue.dma_start(
                out_2[0][4 * quad : 4 * quad + 4, :].bitcast(I32),
                o_scales[32 * quad : 32 * quad + 4, :].bitcast(I32),
            )
